import numpy as np
CORES = [4,12,20,28,36,44,52,60,132,140,148,156,164,172,180,188]
N = 16
GROUPS = [[0,1,2,3,4,5,6,7],[8,9,10,11,12,13,14,15]]
def setup_inputs(rng):
    return {"x": rng.standard_normal((N, 128, 128), dtype=np.float32)}
def reference(x):
    y = np.empty((N, 128, 1024), x.dtype)
    for g in GROUPS:
        s = np.concatenate([x[r] for r in g], axis=1)
        for r in g:
            y[r] = s
    return {"y": y}

@@ -1,0 +1,42 @@
+from concourse.bass import DstId, RemoteDMATransfer
+
+SCRATCH = {
+    "land": ("sbuf", [128, 1024], "float32"),
+}
+SEMAPHORES = ["loaded", "sent", "arrived", "stored"]
+
+W = 128
+
+
+def rank_program(g, core, T, topo):
+    if core % 8 not in (4, 6) or topo.chip(core) >= 8:
+        return
+    base = core - core % 8
+    rank = T.rank_of(base + 4)
+    group = [grp for grp in T.tables["GROUPS"] if rank in grp][0]
+    i = group.index(rank)
+    blk = T.land[:, i * W:(i + 1) * W]
+    peers = [T.cores[r] for r in group if r != rank]
+
+    def send(dsts):
+        ids = []
+        for d in dsts:
+            rid, pid = topo.addr(d, core)
+            ids.append(DstId(rid=rid, pnc=pid))
+        g.remote_dma_fused(
+            [RemoteDMATransfer(dst_ids=ids, dma_engine_mask=0xFF, remote_sem=T.sem.arrived,
+                               srcs=[blk], dsts=[blk for _ in dsts])],
+            local_sem=T.sem.sent)
+
+    if core % 8 == 4:
+        g.dma_start(blk, T.x[:]).then_inc(T.sem.loaded, 16)
+        g.wait_ge(T.sem.loaded, 16)
+        send([d for d in peers if topo.same_plane(core, d)] + [base + 6])
+        g.wait_ge(T.sem.sent, 8)
+        g.wait_ge(T.sem.arrived, 8 * 7)
+        g.dma_start(T.y[:], T.land[:]).then_inc(T.sem.stored, 16)
+        g.wait_ge(T.sem.stored, 16)
+    else:
+        g.wait_ge(T.sem.arrived, 8)
+        send([d for d in peers if not topo.same_plane(core, d)])
+        g.wait_ge(T.sem.sent, 8)

@@ -1,42 +1,74 @@
 from concourse.bass import DstId, RemoteDMATransfer
 
 SCRATCH = {
+    "stage": ("dram", [128, 128], "float32"),
     "land": ("sbuf", [128, 1024], "float32"),
 }
 SEMAPHORES = ["loaded", "sent", "arrived", "stored"]
 
 W = 128
+LOW, HIGH = 0x00FF, 0xFF00
 
 
 def rank_program(g, core, T, topo):
-    if core % 8 not in (4, 6) or topo.chip(core) >= 8:
+    role = core % 8
+    if role not in (2, 4, 6, 7):
         return
-    base = core - core % 8
-    rank = T.rank_of(base + 4)
+    chip_base = core - role
+    rank = T.rank_of(chip_base + 4)
+    if rank is None:
+        return
     group = [grp for grp in T.tables["GROUPS"] if rank in grp][0]
-    i = group.index(rank)
-    blk = T.land[:, i * W:(i + 1) * W]
-    peers = [T.cores[r] for r in group if r != rank]
+    where = {}
+    for i, r in enumerate(group):
+        c = T.cores[r]
+        where[(topo.chip(c) // 2, topo.chip(c) % 2)] = (c, i)
+    npairs = len(group) // 2
+    p, b = topo.chip(core) // 2, topo.chip(core) % 2
 
-    def send(dsts):
-        ids = []
-        for d in dsts:
-            rid, pid = topo.addr(d, core)
-            ids.append(DstId(rid=rid, pnc=pid))
-        g.remote_dma_fused(
-            [RemoteDMATransfer(dst_ids=ids, dma_engine_mask=0xFF, remote_sem=T.sem.arrived,
-                               srcs=[blk], dsts=[blk for _ in dsts])],
-            local_sem=T.sem.sent)
+    def dst(d):
+        rid, pid = topo.addr(d, core)
+        return DstId(rid=rid, pnc=pid)
 
-    if core % 8 == 4:
-        g.dma_start(blk, T.x[:]).then_inc(T.sem.loaded, 16)
+    def transfer(dsts, mask, out):
+        return RemoteDMATransfer(dst_ids=[dst(d) for d in dsts], dma_engine_mask=mask, remote_sem=T.sem.arrived,
+                                 srcs=[T.stage[:]], dsts=[out for _ in dsts])
+
+    def block(i):
+        return T.land[:, i * W:(i + 1) * W]
+
+    if role == 4:
+        me = where[(p, b)][1]
+        up = where[((p + 1) % npairs, b)][0]
+        down = where[((p - 1) % npairs, b)][0]
+        g.sync.dma_start(T.stage[:], T.x[:]).then_inc(T.sem.loaded, 16)
+        g.scalar.dma_start(block(me), T.x[:]).then_inc(T.sem.arrived, 16)
         g.wait_ge(T.sem.loaded, 16)
-        send([d for d in peers if topo.same_plane(core, d)] + [base + 6])
-        g.wait_ge(T.sem.sent, 8)
-        g.wait_ge(T.sem.arrived, 8 * 7)
-        g.dma_start(T.y[:], T.land[:]).then_inc(T.sem.stored, 16)
-        g.wait_ge(T.sem.stored, 16)
-    else:
+        g.remote_dma_fused([
+            transfer([up - 4 + 6], 0x000F, T.stage[:]),
+            transfer([down - 4 + 7], 0x00F0, T.stage[:]),
+            transfer([chip_base + 2], HIGH, T.stage[:]),
+        ], local_sem=T.sem.sent)
+        g.sync.wait_ge(T.sem.arrived, 16 + 8 * (len(group) - 1))
+        g.sync.dma_start(T.y[:], T.land[:]).then_inc(T.sem.stored, 16)
+        g.wait_ge(T.sem.sent, 16)
+        g.sync.wait_ge(T.sem.stored, 16)
+        return
+
+    mate = where[(p, 1 - b)][0]
+    if role == 2:
+        far = (p + 2) % npairs
         g.wait_ge(T.sem.arrived, 8)
-        send([d for d in peers if not topo.same_plane(core, d)])
+        g.remote_dma_fused([
+            transfer([mate, where[(far, b)][0], where[(far, 1 - b)][0]], LOW, block(where[(p, b)][1])),
+        ], local_sem=T.sem.sent)
         g.wait_ge(T.sem.sent, 8)
+    else:
+        src_pair = (p - 1) % npairs if role == 6 else (p + 1) % npairs
+        out = block(where[(src_pair, b)][1])
+        g.wait_ge(T.sem.arrived, 4)
+        g.remote_dma_fused([
+            transfer([mate], LOW, out),
+            transfer([chip_base + 4], HIGH, out),
+        ], local_sem=T.sem.sent)
+        g.wait_ge(T.sem.sent, 16)

from concourse.bass import DstId, RemoteDMATransfer

SCRATCH = {
    "stage": ("dram", [128, 128], "float32"),
    "land": ("sbuf", [128, 1024], "float32"),
}
SEMAPHORES = ["loaded", "sent", "arrived", "stored"]

W = 128
LOW, HIGH = 0x00FF, 0xFF00


def rank_program(g, core, T, topo):
    role = core % 8
    if role not in (2, 4, 6, 7):
        return
    chip_base = core - role
    rank = T.rank_of(chip_base + 4)
    if rank is None:
        return
    group = [grp for grp in T.tables["GROUPS"] if rank in grp][0]
    where = {}
    for i, r in enumerate(group):
        c = T.cores[r]
        where[(topo.chip(c) // 2, topo.chip(c) % 2)] = (c, i)
    npairs = len(group) // 2
    p, b = topo.chip(core) // 2, topo.chip(core) % 2

    def dst(d):
        rid, pid = topo.addr(d, core)
        return DstId(rid=rid, pnc=pid)

    def transfer(dsts, mask, out):
        return RemoteDMATransfer(dst_ids=[dst(d) for d in dsts], dma_engine_mask=mask, remote_sem=T.sem.arrived,
                                 srcs=[T.stage[:]], dsts=[out for _ in dsts])

    def block(i):
        return T.land[:, i * W:(i + 1) * W]

    if role == 4:
        me = where[(p, b)][1]
        up = where[((p + 1) % npairs, b)][0]
        down = where[((p - 1) % npairs, b)][0]
        g.sync.dma_start(T.stage[:], T.x[:]).then_inc(T.sem.loaded, 16)
        g.scalar.dma_start(block(me), T.x[:]).then_inc(T.sem.arrived, 16)
        g.wait_ge(T.sem.loaded, 16)
        g.remote_dma_fused([
            transfer([up - 4 + 6], 0x000F, T.stage[:]),
            transfer([down - 4 + 7], 0x00F0, T.stage[:]),
            transfer([chip_base + 2], HIGH, T.stage[:]),
        ], local_sem=T.sem.sent)
        g.sync.wait_ge(T.sem.arrived, 16 + 8 * (len(group) - 1))
        g.sync.dma_start(T.y[:], T.land[:]).then_inc(T.sem.stored, 16)
        g.wait_ge(T.sem.sent, 16)
        g.sync.wait_ge(T.sem.stored, 16)
        return

    mate = where[(p, 1 - b)][0]
    if role == 2:
        far = (p + 2) % npairs
        g.wait_ge(T.sem.arrived, 8)
        g.remote_dma_fused([
            transfer([mate, where[(far, b)][0], where[(far, 1 - b)][0]], LOW, block(where[(p, b)][1])),
        ], local_sem=T.sem.sent)
        g.wait_ge(T.sem.sent, 8)
    else:
        src_pair = (p - 1) % npairs if role == 6 else (p + 1) % npairs
        out = block(where[(src_pair, b)][1])
        g.wait_ge(T.sem.arrived, 4)
        g.remote_dma_fused([
            transfer([mate], LOW, out),
            transfer([chip_base + 4], HIGH, out),
        ], local_sem=T.sem.sent)
        g.wait_ge(T.sem.sent, 16)
